import numpy as np, ml_dtypes
CORES = [122,123,126,250,251,254,378,379,382,506,507,510]
N = 12
TK = 128
def setup_inputs(rng):
    rt = (0.75 * rng.standard_normal((128, 1), dtype=np.float32) + rng.standard_normal((128, N), dtype=np.float32) / 2).astype(ml_dtypes.bfloat16)
    return {"x": rng.standard_normal((N, 128, TK), dtype=np.float32).astype(ml_dtypes.bfloat16), "rt": np.broadcast_to(rt, (N, 128, N)).copy(), "w": rng.standard_normal((N, 128, 128), dtype=np.float32).astype(ml_dtypes.bfloat16)}
def setup_inputs_big(rng):
    d = setup_inputs(rng)
    for k in ("x", "w"): d[k] = (d[k].astype(np.float32) * 1024.0).astype(d[k].dtype)
    return d
def setup_inputs_small(rng):
    d = setup_inputs(rng)
    for k in ("x", "w"): d[k] = (d[k].astype(np.float32) * (1 / 1024.0)).astype(d[k].dtype)
    return d
def reference(x, rt, w):
    X, RT, W = x.astype(np.float64), rt.astype(np.float64), w.astype(np.float64)
    y = np.zeros((N, 128, TK))
    for r in range(N):
        sc = RT[r].T @ X[r]
        g = np.exp(sc - sc.max(axis=0)); g = g / g.sum(axis=0)
        y[r] = sum(g[j] * (W[j].T @ X[r]) for j in range(N))
    return {"y": y.astype(ml_dtypes.bfloat16)}

from concourse.bass import DstId, RemoteDMATransfer
from concourse.mybir import AluOpType, AxisListType, ActivationFunctionType

N = 12
B = 128
PER = 3
NB = N // PER

SCRATCH = {
    "wall": ("sbuf", [128, N * B], "bfloat16"),
    "wd": ("dram", [128, B], "bfloat16"),
    "wr": ("dram", [128, B], "bfloat16"),
    "xs": ("sbuf", [128, B], "bfloat16"),
    "rts": ("sbuf", [128, 16], "bfloat16"),
    "ones": ("sbuf", [128, B], "bfloat16"),
    "ident": ("sbuf", [128, B], "bfloat16"),
    "xt": ("sbuf", [128, B], "bfloat16"),
    "ee": ("sbuf", [128, 16], "float32"),
    "st": ("sbuf", [128, 16], "float32"),
    "dg": ("sbuf", [128, N * B], "bfloat16"),
    "xg": ("sbuf", [128, N * B], "bfloat16"),
    "ys": ("sbuf", [128, B], "bfloat16"),
    "ps": ("psum", [128, 512], "float32"),
    "pt": ("psum", [128, 1024], "bfloat16"),
    "pg0": ("psum", [128, 512], "float32"),
    "pg1": ("psum", [128, 512], "float32"),
    "pg2": ("psum", [128, 512], "float32"),
    "pg3": ("psum", [128, 512], "float32"),
    "py": ("psum", [128, 512], "float32"),
}
SEMAPHORES = (["wdl", "wl", "xl", "rl", "cl", "on", "idn", "sc", "nm", "ex", "rc", "tp", "xts", "ls", "yy", "yc", "yo"]
              + ["d%d" % b for b in range(NB)] + ["m%d" % b for b in range(NB)] + ["c%d" % b for b in range(NB)]
              + ["a%d" % j for j in range(N)])


def _bits(m):
    return [e for e in range(m.bit_length()) if (m >> e) & 1]


def _mask(engines):
    m = 0
    for e in engines:
        m |= 1 << e
    return m


def _roles(core, T, topo):
    by_host = {}
    for c in T.cores:
        by_host.setdefault(topo.host(c), []).append(c)
    mine = by_host[topo.host(core)]
    i = mine.index(core)
    near = far = None
    for lst in by_host.values():
        if core in lst:
            continue
        if topo.same_plane(core, lst[i]):
            near = lst
        elif topo.may_write(core, lst[i]):
            far = lst

    def rot(lst):
        return [lst[(i + d) % len(lst)] for d in range(len(lst))]

    peers = rot(mine)[1:]
    off = _bits(topo.mask(core, far[i]) & topo.mask(core, near[i]))
    on = [e for e in _bits(topo.mask(core, peers[0])) if e not in off]
    return {"peers": peers, "near": rot(near), "far": far[i], "off": off, "on": on}


def _arrivals(core, T, topo):
    arr = {}
    for s in T.cores:
        if s == core:
            continue
        ro = _roles(s, T, topo)
        own, passed = T.rank_of(s), T.rank_of(ro["far"])
        if ro["far"] == core:
            arr[own] = ("cl", 16, 120)
        if core in ro["near"]:
            k = ro["near"].index(core)
            arr[own] = ("a%d" % own, len(ro["off"]), 110 + k)
            arr[passed] = ("a%d" % passed, len(ro["off"]), 210 + k)
        if core in ro["peers"]:
            k = ro["peers"].index(core)
            arr[own] = ("a%d" % own, len(ro["on"]), 100 + k)
            arr[passed] = ("a%d" % passed, len(ro["on"]), 200 + k)
    return arr


def rank_program(g, core, T, topo):
    me = T.rank_of(core)
    if me is None:
        return
    sem = T.sem
    ro = _roles(core, T, topo)
    arr = _arrivals(core, T, topo)
    seq = [me] + sorted(arr, key=lambda j: arr[j][2])
    jc = T.rank_of(ro["far"])
    n_off, n_on = len(ro["off"]), len(ro["on"])
    m_off, m_on = _mask(ro["off"]), _mask(ro["on"])
    te, ve, se, sy = g.tensor, g.vector, g.scalar, g.sync
    mult = AluOpType.mult

    def slot(j):
        return T.wall[:, j * B:(j + 1) * B]

    def fan(src, j, dsts, m):
        ids = []
        for d in dsts:
            rid, pid = topo.addr(d, core)
            ids.append(DstId(rid=rid, pnc=pid))
        return RemoteDMATransfer(dst_ids=ids, dma_engine_mask=m, remote_sem=sem["a%d" % j], srcs=[src],
                                 dsts=[slot(j) for _ in dsts], alu_op=0)

    sy.dma_start(T.wd[:], T.w[:]).then_inc(sem.wdl, 16)
    se.dma_start(T.xs[:], T.x[:]).then_inc(sem.xl, 16)
    sy.dma_start(T.rts[:, 0:N], T.rt[:]).then_inc(sem.rl, 16)
    sy.dma_start(slot(me), T.w[:]).then_inc(sem.wl, 16)

    ve.memset(T.ones[:], 1.0).then_inc(sem.on, 1)
    g.wait_ge(sem.on, 1)
    g.affine_select(T.ident[:], T.ones[:], [[-1, B]], AluOpType.is_equal, 0.0, 0, 1).then_inc(sem.idn, 1)
    g.wait_ge(sem.wdl, 16)
    rid, pid = topo.addr(ro["far"], core)
    g.remote_dma(T.wr[:], T.wd[:], sem["a%d" % me], sem.ls, pid, rid, m_off)
    g.remote_dma_fused([fan(T.wd[:], me, ro["near"], m_off), fan(T.wd[:], me, ro["peers"], m_on)], local_sem=sem.ls)
    g.wait_ge(sem["a%d" % jc], n_off)
    g.remote_dma_fused([fan(T.wr[:], jc, ro["near"], m_off), fan(T.wr[:], jc, ro["peers"], m_on)], local_sem=sem.ls)
    g.wait_ge(sem.ls, 3 * n_off + 2 * n_on)

    sy.wait_ge(sem["a%d" % jc], n_off)
    sy.dma_start(slot(jc), T.wr[:]).then_inc(sem.cl, 16)
    sy.wait_ge(sem.yc, 1)
    sy.dma_start(T.y[:], T.ys[:]).then_inc(sem.yo, 16)
    sy.wait_ge(sem.yo, 16)

    te.wait_ge(sem.xl, 16)
    te.wait_ge(sem.rl, 16)
    te.matmul(T.ps[:, 0:N], T.xs[:], T.rts[:, 0:N], True, True).then_inc(sem.sc, 1)
    te.wait_ge(sem.idn, 1)
    te.transpose(T.pt[:, 0:B], T.xs[:], T.ident[:]).then_inc(sem.tp, 1)
    te.wait_ge(sem.xts, 1)
    for b in range(NB):
        te.wait_ge(sem["d%d" % b], PER)
        te.matmul(T["pg%d" % b][:, 0:PER * B], T.xt[:], T.dg[:, b * PER * B:(b + 1) * PER * B], True, True).then_inc(sem["m%d" % b], 1)
    for p, j in enumerate(seq):
        if p % PER == 0:
            te.wait_ge(sem["c%d" % (p // PER)], 1)
        if j == me:
            te.wait_ge(sem.wl, 16)
        else:
            te.wait_ge(sem[arr[j][0]], arr[j][1])
        mm = te.matmul(T.py[:, 0:B], slot(j), T.xg[:, p * B:(p + 1) * B], p == 0, p == N - 1)
    mm.then_inc(sem.yy, 1)

    def diag(b, on_vector):
        for p in range(b * PER, (b + 1) * PER):
            j = seq[p]
            if on_vector:
                ve.tensor_scalar(T.dg[:, p * B:(p + 1) * B], T.ident[:], T.ee[:, j:j + 1], None, mult).then_inc(sem["d%d" % b], 1)
            else:
                se.activation(T.dg[:, p * B:(p + 1) * B], T.ident[:], ActivationFunctionType.Copy,
                              scale=T.ee[:, j:j + 1]).then_inc(sem["d%d" % b], 1)

    def empty(b, on_vector):
        out, in_ = T.xg[:, b * PER * B:(b + 1) * PER * B], T["pg%d" % b][:, 0:PER * B]
        if on_vector:
            ve.wait_ge(sem["m%d" % b], 1)
            ve.tensor_copy(out, in_).then_inc(sem["c%d" % b], 1)
        else:
            se.wait_ge(sem["m%d" % b], 1)
            se.activation(out, in_, ActivationFunctionType.Copy).then_inc(sem["c%d" % b], 1)

    ve.wait_ge(sem.sc, 1)
    ve.tensor_reduce(T.st[:, 0:1], T.ps[:, 0:N], axis=AxisListType.X, op=AluOpType.max, negate=True).then_inc(sem.nm, 1)
    se.wait_ge(sem.nm, 1)
    se.activation(T.ee[:, 0:N], T.ps[:, 0:N], ActivationFunctionType.Exp, bias=T.st[:, 0:1], scale=1.0,
                  accum_out=T.st[:, 4:5]).then_inc(sem.ex, 1)

    se.wait_ge(sem.ex, 1)
    se.wait_ge(sem.idn, 1)
    diag(0, False)
    empty(0, False)
    empty(2, False)

    ve.wait_ge(sem.ex, 1)
    ve.reciprocal(T.st[:, 8:9], T.st[:, 4:5]).then_inc(sem.rc, 1)
    ve.wait_ge(sem.rc, 1)
    ve.wait_ge(sem.tp, 1)
    ve.tensor_scalar(T.xt[:], T.pt[:, 0:B], T.st[:, 8:9], None, mult).then_inc(sem.xts, 1)
    ve.wait_ge(sem.idn, 1)
    diag(1, True)
    diag(2, True)
    diag(3, True)
    empty(1, True)
    empty(3, True)
    ve.wait_ge(sem.yy, 1)
    ve.tensor_copy(T.ys[:], T.py[:, 0:B]).then_inc(sem.yc, 1)
